import numpy as np
import ml_dtypes


def mxq(x, axis, fmt="e4m3"):
    dtype, down = {"e4m3": (ml_dtypes.float8_e4m3fn, 7), "e5m2": (ml_dtypes.float8_e5m2, 14)}[fmt]
    v = np.moveaxis(np.asarray(x, np.float32).astype(ml_dtypes.bfloat16).astype(np.float64), axis, -1)
    blocks = v.reshape(v.shape[:-1] + (-1, 32))
    amax = np.abs(blocks).max(-1, keepdims=True)
    byte = np.maximum(np.where(amax > 0, np.frexp(amax)[1] - 1 + 127, 0) - down, 1)
    scale = np.exp2(byte - 127.0)
    codes = (blocks / scale).astype(np.float32).astype(dtype).astype(np.float64)
    return np.moveaxis((codes * scale).reshape(v.shape), -1, axis)


WIDE = False


def mx_kscale(k):
    if not WIDE:
        return np.ones(k)
    levels = np.array([10, -10, 5, -5, 0])
    if k % 512:
        return np.exp2(np.random.permutation(np.resize(levels, k // 32))).repeat(32)
    a = np.empty((k // 512, 16))
    for p in range(k // 512):
        a[p, :8] = np.random.permutation(np.resize(levels, 8))
        for g in range(8):
            far = levels[np.abs(levels - a[p, g]) >= 10]
            a[p, g + 8] = far[np.random.randint(len(far))]
    return np.exp2(a.ravel()).repeat(32)


def f64(x):
    return np.asarray(x).astype(np.float64)


def striped(idx):
    return np.tile(idx.reshape(-1, 16).T, (8, 1)).astype(np.uint16)


def unstriped(offs):
    return offs[:16].T.reshape(-1).astype(np.int64)


def striped8(idx):
    return np.concatenate([x.reshape(-1, 16).T for x in idx]).astype(np.uint16)


def runs(offs, k):
    lists = np.stack([offs[16 * r : 16 * r + 16].T.reshape(-1) for r in range(8)]).astype(np.int64)
    return lists[np.arange(k) % 512 // 64]


def pack_weight(w):
    k, n = w.shape
    w = f64(np.asarray(w, np.float32).astype(ml_dtypes.bfloat16)).reshape(k // 32, 32, n)
    amax = np.abs(w).max(1)
    byte = np.clip(np.where(amax > 0, np.frexp(amax)[1] - 1 + 127 - 7, 1), 1, 254)
    scaled = (w * np.exp2(127.0 - byte)[:, None, :]).reshape(k, n).astype(np.float32)
    words = np.ascontiguousarray(scaled.reshape(k // 512, 128, 4, n).transpose(0, 1, 3, 2)).astype(ml_dtypes.float8_e4m3fn).view(np.uint8)
    return words, np.ascontiguousarray(byte.astype(np.uint8).reshape(k // 512, 16, n))


def unpack_weight(words, scales):
    g, p, n, _ = words.shape
    vals = np.ascontiguousarray(words).view(ml_dtypes.float8_e4m3fn).astype(np.float64) * np.repeat(np.exp2(scales.astype(np.float64) - 127.0), 8, axis=1)[..., None]
    return vals.transpose(0, 1, 3, 2).reshape(g * 512, n)


E2M1 = np.array([0.0, 0.5, 1.0, 1.5, 2.0, 3.0, 4.0, 6.0, -0.0, -0.5, -1.0, -1.5, -2.0, -3.0, -4.0, -6.0])


def pack_fp4(w):
    k, n = w.shape
    w = f64(np.asarray(w, np.float32).astype(ml_dtypes.bfloat16)).reshape(k // 32, 32, n)
    amax = np.abs(w).max(1)
    mant, ex = np.frexp(amax / 6.0)
    byte = np.clip(np.where(amax > 0, np.where(mant > 0.5, ex, ex - 1) + 127, 1), 1, 254)
    scaled = (w * np.exp2(127.0 - byte)[:, None, :]).reshape(k, n).astype(np.float32)
    c = np.ascontiguousarray(scaled.reshape(k // 512, 128, 4, n).transpose(0, 1, 3, 2)).astype(ml_dtypes.float4_e2m1fn).view(np.uint8) & 0xF
    words = (c[..., 0::2] | (c[..., 1::2] << 4)).reshape(k // 512, 128, 2 * n)
    return np.ascontiguousarray(words), np.ascontiguousarray(byte.astype(np.uint8).reshape(k // 512, 16, n))


def unpack_fp4(words, scales):
    g, _, n = scales.shape
    words = np.ascontiguousarray(words).reshape(g, 128, n, 2)
    nib = np.empty((g, 128, n, 4), np.uint8)
    nib[..., 0::2] = words & 0xF
    nib[..., 1::2] = words >> 4
    vals = E2M1[nib] * np.repeat(np.exp2(scales.astype(np.float64) - 127.0), 8, axis=1)[..., None]
    return vals.transpose(0, 1, 3, 2).reshape(g * 512, n)


K, T, S, H, G, U = 512, 2048, 256, 512, 2048, 512


def setup_inputs():
    n = np.random.standard_normal
    s = mx_kscale(K)[:, None]
    packed_xT = pack_weight(n((K, T)) * s)
    packed_w1 = pack_fp4(n((K, H)) / np.sqrt(K) / s)
    packed_dT = pack_weight(n((K, G)) / s)
    perm = np.random.permutation(U)
    return {
        "x_words": packed_xT[0],
        "x_scales": packed_xT[1],
        "w1_words": packed_w1[0],
        "w1_scales": packed_w1[1],
        "gs": (np.random.uniform(0.5, 1.5, (K, 1)) * s).astype(np.float32),
        "d_words": packed_dT[0],
        "d_scales": packed_dT[1],
        "offs": striped8(np.random.randint(0, T, (8, S))),
        "ka": striped8(np.random.randint(0, G, (8, H))),
        "kb": striped8(np.random.randint(0, G, (8, H))),
        "n1": striped(perm[:S]),
        "n2": striped(perm[S:]),
        "n3": striped(np.random.permutation(S)),
    }


def reference(x_words, x_scales, w1_words, w1_scales, gs, d_words, d_scales, offs, ka, kb, n1, n2, n3):
    d_ka = unpack_weight(d_words, d_scales)[np.arange(K)[:, None], runs(ka, K)]
    xq = unpack_weight(x_words, x_scales)[np.arange(K)[:, None], runs(offs, K)]
    y = unpack_fp4(w1_words, w1_scales).T @ xq
    z = f64(gs) * y
    zq = mxq(z, 0, "e4m3")
    d_kb = unpack_weight(d_words, d_scales)[np.arange(K)[:, None], runs(kb, K)]
    h = 0.0625 * (d_ka.T @ zq + d_kb.T @ zq)
    nw = h - h[:, unstriped(n3)]
    ph = np.zeros((H, U))
    ph[:, unstriped(n1)] = h
    out = ph.copy()
    out[:, unstriped(n2)] = nw
    return out

@@ -1,0 +1,203 @@
+from contextlib import ExitStack
+
+import concourse.mybir as mybir
+
+F32 = mybir.dt.float32
+BF16 = mybir.dt.bfloat16
+I32 = mybir.dt.int32
+U32 = mybir.dt.uint32
+U16 = mybir.dt.uint16
+U8 = mybir.dt.uint8
+FP8X4 = mybir.dt.float8_e4m3fn_x4
+FP4X4 = mybir.dt.float4_e2m1fn_x4
+COPY = mybir.ActivationFunctionType.Copy
+MULT = mybir.AluOpType.mult
+SUBTRACT = mybir.AluOpType.subtract
+
+P = 128
+PACK = 4
+K = 512
+TABLE = 2048
+S = 256
+H = 512
+U = 512
+PER_COL = 16
+HALF = 128
+PICK = 256
+H_SCALE = 0.0625
+
+FLOPS = 2 * K * H * S * 3
+
+
+def tile_picked_hdaqipagq_none_p_kernel(
+    tc, x_words, x_scales, w1_words, w1_scales, gs, d_words, d_scales, offs, ka, kb, n1, n2, n3, out
+):
+    nc = tc.nc
+    with ExitStack() as ctx:
+        keep = ctx.enter_context(tc.tile_pool(name="keep", bufs=1))
+        psum = ctx.enter_context(tc.psum_pool(name="psum", bufs=1))
+
+        def load_list(src, name):
+            t = keep.tile(list(src.shape), U16, name=name)
+            nc.sync.dma_start(out=t[:], in_=src)
+            return t
+
+        def load_words(src, name):
+            t = keep.tile([P, TABLE], I32, name=name, tag=name, align_bytes=64)
+            nc.sync.dma_start(out=t[:], in_=src[0].rearrange("p n t -> p (n t)").bitcast(I32))
+            return t
+
+        def load_scale_window(src, name, zero_engine):
+            t = keep.tile([P, TABLE], U8, name=name, align_bytes=64)
+            zero_engine.memset(t[:].bitcast(I32), 0)
+            nc.scalar.dma_start(out=t[0:P:8, :].bitcast(I32), in_=src[0].bitcast(I32))
+            return t
+
+        def place_scales(picked, plane, queue):
+            nc.vector.tensor_copy(out=plane[:].bitcast(I32), in_=picked[:].bitcast(I32))
+            for i in range(1, 4):
+                queue.dma_start(out=plane[i:P:32, :].bitcast(I32), in_=picked[8 * i : P : 32, :].bitcast(I32))
+
+        def entries(lst, first, count):
+            return lst[:, first // PER_COL : (first + count) // PER_COL]
+
+        offs_t = load_list(offs, "offs_t")
+        ka_t = load_list(ka, "ka_t")
+        dw_win = load_words(d_words, "dw_win")
+        kb_t = load_list(kb, "kb_t")
+        n1_t = load_list(n1, "n1_t")
+        n3_t = load_list(n3, "n3_t")
+        n2_t = load_list(n2, "n2_t")
+        xw_win = load_words(x_words, "xw_win")
+        xs_win = load_scale_window(x_scales, "xs_win", nc.vector)
+        ds_win = load_scale_window(d_scales, "ds_win", nc.vector)
+
+        w1s_raw = keep.tile([P, H], U8, name="w1s_raw", align_bytes=64)
+        nc.gpsimd.memset(w1s_raw[:].bitcast(I32), 0)
+        for i in range(4):
+            nc.gpsimd.dma_start(out=w1s_raw[i:P:32, :].bitcast(I32), in_=w1_scales[0, i:16:4, :].bitcast(I32))
+        w1w_raw = keep.tile([P, 2 * H], U8, name="w1w_raw", align_bytes=64)
+        nc.gpsimd.dma_start(out=w1w_raw[:].bitcast(I32), in_=w1_words[0].bitcast(I32))
+        gs4 = keep.tile([P, PACK], F32, name="gs4")
+        nc.gpsimd.dma_start(out=gs4[:], in_=gs.rearrange("(p t) o -> p (t o)", t=PACK))
+
+        picked0 = keep.tile([P, S + 2 * PICK], U8, name="picked0", tag="bytes_a", align_bytes=64)
+        nc.vector.tensor_copy(out=picked0[:, 0:S], in_=xs_win[:].indirect(offs_t[:]))
+        nc.vector.tensor_copy(out=picked0[:, S : S + PICK], in_=ds_win[:].indirect(entries(ka_t, 0, PICK)))
+        nc.vector.tensor_copy(out=picked0[:, S + PICK : S + 2 * PICK], in_=ds_win[:].indirect(entries(kb_t, 0, PICK)))
+        plane0 = keep.tile([P, S + 2 * PICK], U8, name="plane0", tag="bytes_b", align_bytes=64)
+        place_scales(picked0, plane0, nc.scalar)
+
+        def pick_words(window, lst, first, name, tag):
+            picked = keep.tile([P, PICK], I32, name=name, tag=tag, align_bytes=64)
+            nc.vector.tensor_copy(out=picked[:].bitcast(U32), in_=window[:].bitcast(U32).indirect(entries(lst, first, PICK)))
+            return picked
+
+        ka_pick = pick_words(dw_win, ka_t, 0, "ka_pick0", "ka_pick")
+        xw_pick = pick_words(xw_win, offs_t, 0, "xw_pick", "xw_pick")
+        kb_pick = pick_words(dw_win, kb_t, 0, "kb_pick0", "xw_win")
+        dw_pick = (ka_pick, kb_pick)
+
+        w1w = keep.tile([P, 2 * H], U8, name="w1w", align_bytes=64)
+        nc.scalar.copy(
+            out=w1w[:].bitcast(U16).rearrange("p (t m) -> p t m", t=PACK),
+            in_=w1w_raw[:].bitcast(U16).rearrange("p (m t) -> p t m", t=PACK),
+        )
+        w1s = keep.tile([P, H], U8, name="w1s", align_bytes=64)
+        nc.vector.tensor_copy(
+            out=w1s[:].rearrange("p (t m) -> p t m", t=PACK),
+            in_=w1s_raw[:].rearrange("p (m t) -> p t m", t=PACK),
+        )
+
+        pages = [keep.tile([P, U], F32, name=f"page{b}") for b in range(H // P)]
+        hs = [keep.tile([P, S], F32, name=f"h{b}") for b in range(H // P)]
+
+        zq = keep.tile([P, S], I32, name="zq", align_bytes=64)
+        zs = keep.tile([P, S], U8, name="zs", align_bytes=64)
+
+        def second_product(acc, words, plane, first_scale, bb, cols):
+            for m in range(2):
+                at = m * PICK + bb * P
+                nc.tensor.matmul_mx(
+                    out=acc[:],
+                    lhsT=words[m][:, bb * P : (bb + 1) * P].bitcast(FP8X4),
+                    lhsT_scale=plane[:, first_scale + at : first_scale + at + P],
+                    rhs=zq[:, cols].bitcast(FP8X4),
+                    rhs_scale=zs[:, cols],
+                    start=(m == 0),
+                    stop=(m == 1),
+                )
+
+        def finish(b):
+            fetched = keep.tile([P, S], F32, name=f"fetched{b}")
+            for hh in range(S // HALF):
+                nc.scalar.activation(
+                    out=fetched[:, hh * HALF : (hh + 1) * HALF],
+                    in_=hs[b][:].indirect(entries(n3_t, hh * HALF, HALF)),
+                    func=COPY,
+                )
+            nw = keep.tile([P, S], F32, name=f"nw{b}")
+            nc.vector.tensor_tensor(out=nw[:], in0=hs[b][:], in1=fetched[:], op=SUBTRACT)
+            return nw
+
+        def put_nw(b, nw):
+            nc.scalar.activation(out=pages[b][:].indirect(n2_t[:]), in_=nw[:], func=COPY)
+            nc.sync.dma_start(out=out[b * P : (b + 1) * P, :], in_=pages[b][:])
+
+        ys = []
+        for hh in range(S // HALF):
+            cols = slice(hh * HALF, (hh + 1) * HALF)
+            y = psum.tile([P, PACK, HALF], F32, name=f"y{hh}")
+            for t in range(PACK):
+                nc.tensor.matmul_mx(
+                    out=y[:, t, :],
+                    lhsT=w1w[:, 2 * P * t : 2 * P * (t + 1)].bitcast(FP4X4),
+                    lhsT_scale=w1s[:, P * t : P * (t + 1)],
+                    rhs=xw_pick[:, cols].bitcast(FP8X4),
+                    rhs_scale=plane0[:, cols],
+                    start=True,
+                    stop=True,
+                )
+            ys.append(y)
+        for hh in range(S // HALF):
+            cols = slice(hh * HALF, (hh + 1) * HALF)
+            zb = keep.tile([P, HALF * PACK], BF16, name=f"zb{hh}", align_bytes=64)
+            nc.vector.tensor_tensor(
+                out=zb[:].rearrange("p (j t) -> p j t", t=PACK),
+                in0=ys[hh][:].rearrange("p t j -> p j t"),
+                in1=gs4[:].unsqueeze(1).to_broadcast([P, HALF, PACK]),
+                op=MULT,
+            )
+            nc.vector.quantize_mx(out=zq[:, cols].bitcast(FP8X4), scales=zs[:, cols], in_=zb[:])
+            for b in range(PICK // P):
+                acc = psum.tile([P, HALF], F32, name=f"acc{b}_{hh}")
+                second_product(acc, dw_pick, plane0, S, b, cols)
+                if hh == 0:
+                    nc.scalar.activation(out=hs[b][:, cols], in_=acc[:], func=COPY, scale=H_SCALE)
+                else:
+                    nc.vector.tensor_scalar(out=hs[b][:, cols], in0=acc[:], scalar1=H_SCALE, scalar2=None, op0=MULT)
+                nc.scalar.activation(
+                    out=pages[b][:].indirect(entries(n1_t, hh * HALF, HALF)), in_=hs[b][:, cols], func=COPY
+                )
+        picked1 = keep.tile([P, 2 * PICK], U8, name="picked1", tag="bytes_b", align_bytes=64)
+        nc.vector.tensor_copy(out=picked1[:, 0:PICK], in_=ds_win[:].indirect(entries(ka_t, PICK, PICK)))
+        nc.vector.tensor_copy(out=picked1[:, PICK : 2 * PICK], in_=ds_win[:].indirect(entries(kb_t, PICK, PICK)))
+        plane1 = keep.tile([P, 2 * PICK], U8, name="plane1", tag="bytes_a", align_bytes=64)
+        place_scales(picked1, plane1, nc.sync)
+        nws = [finish(b) for b in range(PICK // P)]
+        for b in range(PICK // P):
+            put_nw(b, nws[b])
+        dw_pick = (
+            pick_words(dw_win, ka_t, PICK, "ka_pick1", "ka_pick"),
+            pick_words(dw_win, kb_t, PICK, "kb_pick1", "xw_win"),
+        )
+        nws = []
+        for bb in range(PICK // P):
+            b = PICK // P + bb
+            acc = psum.tile([P, S], F32, name=f"acc{b}")
+            second_product(acc, dw_pick, plane1, 0, bb, slice(0, S))
+            nc.vector.tensor_scalar(out=hs[b][:], in0=acc[:], scalar1=H_SCALE, scalar2=None, op0=MULT)
+            nws.append(finish(b))
+            nc.scalar.activation(out=pages[b][:].indirect(n1_t[:]), in_=hs[b][:], func=COPY)
+        for bb in range(PICK // P):
+            put_nw(PICK // P + bb, nws[bb])

@@ -47,10 +47,10 @@ def tile_picked_hdaqipagq_none_p_kernel(
             nc.sync.dma_start(out=t[:], in_=src[0].rearrange("p n t -> p (n t)").bitcast(I32))
             return t
 
-        def load_scale_window(src, name, zero_engine):
+        def load_scale_window(src, name, queue):
             t = keep.tile([P, TABLE], U8, name=name, align_bytes=64)
-            zero_engine.memset(t[:].bitcast(I32), 0)
-            nc.scalar.dma_start(out=t[0:P:8, :].bitcast(I32), in_=src[0].bitcast(I32))
+            nc.vector.memset(t[:].bitcast(I32), 0)
+            queue.dma_start(out=t[0:P:8, :].bitcast(I32), in_=src[0].bitcast(I32))
             return t
 
         def place_scales(picked, plane, queue):
@@ -63,23 +63,29 @@ def tile_picked_hdaqipagq_none_p_kernel(
 
         offs_t = load_list(offs, "offs_t")
         ka_t = load_list(ka, "ka_t")
-        dw_win = load_words(d_words, "dw_win")
         kb_t = load_list(kb, "kb_t")
+        xs_win = load_scale_window(x_scales, "xs_win", nc.sync)
+        ds_win = load_scale_window(d_scales, "ds_win", nc.scalar)
+        dw_win = load_words(d_words, "dw_win")
+        w1w_raw = keep.tile([P, 2 * H], U8, name="w1w_raw", align_bytes=64)
+        nc.sync.dma_start(out=w1w_raw[:].bitcast(I32), in_=w1_words[0].bitcast(I32))
+        xw_win = load_words(x_words, "xw_win")
+        gs4 = keep.tile([P, PACK], F32, name="gs4")
+        nc.sync.dma_start(out=gs4[:], in_=gs.rearrange("(p t) o -> p (t o)", t=PACK))
         n1_t = load_list(n1, "n1_t")
         n3_t = load_list(n3, "n3_t")
         n2_t = load_list(n2, "n2_t")
-        xw_win = load_words(x_words, "xw_win")
-        xs_win = load_scale_window(x_scales, "xs_win", nc.vector)
-        ds_win = load_scale_window(d_scales, "ds_win", nc.vector)
 
         w1s_raw = keep.tile([P, H], U8, name="w1s_raw", align_bytes=64)
-        nc.gpsimd.memset(w1s_raw[:].bitcast(I32), 0)
+        nc.vector.memset(w1s_raw[:].bitcast(I32), 0)
         for i in range(4):
-            nc.gpsimd.dma_start(out=w1s_raw[i:P:32, :].bitcast(I32), in_=w1_scales[0, i:16:4, :].bitcast(I32))
-        w1w_raw = keep.tile([P, 2 * H], U8, name="w1w_raw", align_bytes=64)
-        nc.gpsimd.dma_start(out=w1w_raw[:].bitcast(I32), in_=w1_words[0].bitcast(I32))
-        gs4 = keep.tile([P, PACK], F32, name="gs4")
-        nc.gpsimd.dma_start(out=gs4[:], in_=gs.rearrange("(p t) o -> p (t o)", t=PACK))
+            nc.scalar.dma_start(out=w1s_raw[i:P:32, :].bitcast(I32), in_=w1_scales[0, i:16:4, :].bitcast(I32))
+
+        w1w = keep.tile([P, 2 * H], U8, name="w1w", align_bytes=64)
+        nc.scalar.copy(
+            out=w1w[:].bitcast(U16).rearrange("p (t m) -> p t m", t=PACK),
+            in_=w1w_raw[:].bitcast(U16).rearrange("p (m t) -> p t m", t=PACK),
+        )
 
         picked0 = keep.tile([P, S + 2 * PICK], U8, name="picked0", tag="bytes_a", align_bytes=64)
         nc.vector.tensor_copy(out=picked0[:, 0:S], in_=xs_win[:].indirect(offs_t[:]))
@@ -87,6 +93,12 @@ def tile_picked_hdaqipagq_none_p_kernel(
         nc.vector.tensor_copy(out=picked0[:, S + PICK : S + 2 * PICK], in_=ds_win[:].indirect(entries(kb_t, 0, PICK)))
         plane0 = keep.tile([P, S + 2 * PICK], U8, name="plane0", tag="bytes_b", align_bytes=64)
         place_scales(picked0, plane0, nc.scalar)
+
+        w1s = keep.tile([P, H], U8, name="w1s", align_bytes=64)
+        nc.vector.tensor_copy(
+            out=w1s[:].rearrange("p (t m) -> p t m", t=PACK),
+            in_=w1s_raw[:].rearrange("p (m t) -> p t m", t=PACK),
+        )
 
         def pick_words(window, lst, first, name, tag):
             picked = keep.tile([P, PICK], I32, name=name, tag=tag, align_bytes=64)
@@ -97,17 +109,6 @@ def tile_picked_hdaqipagq_none_p_kernel(
         xw_pick = pick_words(xw_win, offs_t, 0, "xw_pick", "xw_pick")
         kb_pick = pick_words(dw_win, kb_t, 0, "kb_pick0", "xw_win")
         dw_pick = (ka_pick, kb_pick)
-
-        w1w = keep.tile([P, 2 * H], U8, name="w1w", align_bytes=64)
-        nc.scalar.copy(
-            out=w1w[:].bitcast(U16).rearrange("p (t m) -> p t m", t=PACK),
-            in_=w1w_raw[:].bitcast(U16).rearrange("p (m t) -> p t m", t=PACK),
-        )
-        w1s = keep.tile([P, H], U8, name="w1s", align_bytes=64)
-        nc.vector.tensor_copy(
-            out=w1s[:].rearrange("p (t m) -> p t m", t=PACK),
-            in_=w1s_raw[:].rearrange("p (m t) -> p t m", t=PACK),
-        )
 
         pages = [keep.tile([P, U], F32, name=f"page{b}") for b in range(H // P)]
         hs = [keep.tile([P, S], F32, name=f"h{b}") for b in range(H // P)]

@@ -47,10 +47,10 @@ def tile_picked_hdaqipagq_none_p_kernel(
             nc.sync.dma_start(out=t[:], in_=src[0].rearrange("p n t -> p (n t)").bitcast(I32))
             return t
 
-        def load_scale_window(src, name, queue):
+        def load_scale_window(src, name, zero_engine):
             t = keep.tile([P, TABLE], U8, name=name, align_bytes=64)
-            nc.vector.memset(t[:].bitcast(I32), 0)
-            queue.dma_start(out=t[0:P:8, :].bitcast(I32), in_=src[0].bitcast(I32))
+            zero_engine.memset(t[:].bitcast(I32), 0)
+            nc.sync.dma_start(out=t[0:P:8, :].bitcast(I32), in_=src[0].bitcast(I32))
             return t
 
         def place_scales(picked, plane, queue):
@@ -61,25 +61,24 @@ def tile_picked_hdaqipagq_none_p_kernel(
         def entries(lst, first, count):
             return lst[:, first // PER_COL : (first + count) // PER_COL]
 
+        w1w_raw = keep.tile([P, 2 * H], U8, name="w1w_raw", align_bytes=64)
+        nc.sync.dma_start(out=w1w_raw[:].bitcast(I32), in_=w1_words[0].bitcast(I32))
         offs_t = load_list(offs, "offs_t")
         ka_t = load_list(ka, "ka_t")
         kb_t = load_list(kb, "kb_t")
-        xs_win = load_scale_window(x_scales, "xs_win", nc.sync)
-        ds_win = load_scale_window(d_scales, "ds_win", nc.scalar)
+        xs_win = load_scale_window(x_scales, "xs_win", nc.vector)
+        ds_win = load_scale_window(d_scales, "ds_win", nc.gpsimd)
         dw_win = load_words(d_words, "dw_win")
-        w1w_raw = keep.tile([P, 2 * H], U8, name="w1w_raw", align_bytes=64)
-        nc.sync.dma_start(out=w1w_raw[:].bitcast(I32), in_=w1_words[0].bitcast(I32))
+        w1s_raw = keep.tile([P, H], U8, name="w1s_raw", align_bytes=64)
+        nc.vector.memset(w1s_raw[:].bitcast(I32), 0)
+        for i in range(4):
+            nc.sync.dma_start(out=w1s_raw[i:P:32, :].bitcast(I32), in_=w1_scales[0, i:16:4, :].bitcast(I32))
         xw_win = load_words(x_words, "xw_win")
         gs4 = keep.tile([P, PACK], F32, name="gs4")
         nc.sync.dma_start(out=gs4[:], in_=gs.rearrange("(p t) o -> p (t o)", t=PACK))
         n1_t = load_list(n1, "n1_t")
         n3_t = load_list(n3, "n3_t")
         n2_t = load_list(n2, "n2_t")
-
-        w1s_raw = keep.tile([P, H], U8, name="w1s_raw", align_bytes=64)
-        nc.vector.memset(w1s_raw[:].bitcast(I32), 0)
-        for i in range(4):
-            nc.scalar.dma_start(out=w1s_raw[i:P:32, :].bitcast(I32), in_=w1_scales[0, i:16:4, :].bitcast(I32))
 
         w1w = keep.tile([P, 2 * H], U8, name="w1w", align_bytes=64)
         nc.scalar.copy(
@@ -92,7 +91,7 @@ def tile_picked_hdaqipagq_none_p_kernel(
         nc.vector.tensor_copy(out=picked0[:, S : S + PICK], in_=ds_win[:].indirect(entries(ka_t, 0, PICK)))
         nc.vector.tensor_copy(out=picked0[:, S + PICK : S + 2 * PICK], in_=ds_win[:].indirect(entries(kb_t, 0, PICK)))
         plane0 = keep.tile([P, S + 2 * PICK], U8, name="plane0", tag="bytes_b", align_bytes=64)
-        place_scales(picked0, plane0, nc.scalar)
+        place_scales(picked0, plane0, nc.sync)
 
         w1s = keep.tile([P, H], U8, name="w1s", align_bytes=64)
         nc.vector.tensor_copy(
@@ -111,7 +110,9 @@ def tile_picked_hdaqipagq_none_p_kernel(
         dw_pick = (ka_pick, kb_pick)
 
         pages = [keep.tile([P, U], F32, name=f"page{b}") for b in range(H // P)]
-        hs = [keep.tile([P, S], F32, name=f"h{b}") for b in range(H // P)]
+        hs = [keep.tile([P, S + PER_COL], F32, name=f"h{b}") for b in range(H // P)]
+        for h in hs:
+            nc.gpsimd.memset(h[:, S : S + PER_COL], 0.0)
 
         zq = keep.tile([P, S], I32, name="zq", align_bytes=64)
         zs = keep.tile([P, S], U8, name="zs", align_bytes=64)
@@ -131,14 +132,9 @@ def tile_picked_hdaqipagq_none_p_kernel(
 
         def finish(b):
             fetched = keep.tile([P, S], F32, name=f"fetched{b}")
-            for hh in range(S // HALF):
-                nc.scalar.activation(
-                    out=fetched[:, hh * HALF : (hh + 1) * HALF],
-                    in_=hs[b][:].indirect(entries(n3_t, hh * HALF, HALF)),
-                    func=COPY,
-                )
+            nc.scalar.activation(out=fetched[:], in_=hs[b][:].indirect(n3_t[:]), func=COPY)
             nw = keep.tile([P, S], F32, name=f"nw{b}")
-            nc.vector.tensor_tensor(out=nw[:], in0=hs[b][:], in1=fetched[:], op=SUBTRACT)
+            nc.vector.tensor_tensor(out=nw[:], in0=hs[b][:, 0:S], in1=fetched[:], op=SUBTRACT)
             return nw
 
         def put_nw(b, nw):
@@ -162,7 +158,7 @@ def tile_picked_hdaqipagq_none_p_kernel(
             ys.append(y)
         for hh in range(S // HALF):
             cols = slice(hh * HALF, (hh + 1) * HALF)
-            zb = keep.tile([P, HALF * PACK], BF16, name=f"zb{hh}", align_bytes=64)
+            zb = keep.tile([P, HALF * PACK], BF16, name=f"zb{hh}", tag="zb", align_bytes=64)
             nc.vector.tensor_tensor(
                 out=zb[:].rearrange("p (j t) -> p j t", t=PACK),
                 in0=ys[hh][:].rearrange("p t j -> p j t"),
@@ -173,7 +169,7 @@ def tile_picked_hdaqipagq_none_p_kernel(
             for b in range(PICK // P):
                 acc = psum.tile([P, HALF], F32, name=f"acc{b}_{hh}")
                 second_product(acc, dw_pick, plane0, S, b, cols)
-                if hh == 0:
+                if hh == 0 and b == 0:
                     nc.scalar.activation(out=hs[b][:, cols], in_=acc[:], func=COPY, scale=H_SCALE)
                 else:
                     nc.vector.tensor_scalar(out=hs[b][:, cols], in0=acc[:], scalar1=H_SCALE, scalar2=None, op0=MULT)
@@ -197,8 +193,8 @@ def tile_picked_hdaqipagq_none_p_kernel(
             b = PICK // P + bb
             acc = psum.tile([P, S], F32, name=f"acc{b}")
             second_product(acc, dw_pick, plane1, 0, bb, slice(0, S))
-            nc.vector.tensor_scalar(out=hs[b][:], in0=acc[:], scalar1=H_SCALE, scalar2=None, op0=MULT)
+            nc.vector.tensor_scalar(out=hs[b][:, 0:S], in0=acc[:], scalar1=H_SCALE, scalar2=None, op0=MULT)
             nws.append(finish(b))
-            nc.scalar.activation(out=pages[b][:].indirect(n1_t[:]), in_=hs[b][:], func=COPY)
+            nc.scalar.activation(out=pages[b][:].indirect(n1_t[:]), in_=hs[b][:, 0:S], func=COPY)
         for bb in range(PICK // P):
             put_nw(PICK // P + bb, nws[bb])

@@ -134,7 +134,7 @@ def tile_picked_hdaqipagq_none_p_kernel(
             fetched = keep.tile([P, S], F32, name=f"fetched{b}")
             nc.scalar.activation(out=fetched[:], in_=hs[b][:].indirect(n3_t[:]), func=COPY)
             nw = keep.tile([P, S], F32, name=f"nw{b}")
-            nc.vector.tensor_tensor(out=nw[:], in0=hs[b][:, 0:S], in1=fetched[:], op=SUBTRACT)
+            nc.gpsimd.tensor_tensor(out=nw[:], in0=hs[b][:, 0:S], in1=fetched[:], op=SUBTRACT)
             return nw
 
         def put_nw(b, nw):

@@ -22,8 +22,14 @@ S = 256
 H = 512
 U = 512
 PER_COL = 16
+QUADRANT = 32
+ROWS_PER_QUADRANT = 4
+SCALE_ROWS = 16
+BLOCK_PARTS = 8
+FP4_BYTES = 2
 HALF = 128
 PICK = 256
+BLOCKS_PER_SET = PICK // P
 H_SCALE = 0.0625
 
 FLOPS = 2 * K * H * S * 3
@@ -38,30 +44,42 @@ def tile_picked_hdaqipagq_none_p_kernel(
         psum = ctx.enter_context(tc.psum_pool(name="psum", bufs=1))
 
         def load_list(src, name):
-            t = keep.tile(list(src.shape), U16, name=name)
-            nc.sync.dma_start(out=t[:], in_=src)
-            return t
+            tile = keep.tile(list(src.shape), U16, name=name)
+            nc.sync.dma_start(out=tile[:], in_=src)
+            return tile
 
         def load_words(src, name):
-            t = keep.tile([P, TABLE], I32, name=name, tag=name, align_bytes=64)
-            nc.sync.dma_start(out=t[:], in_=src[0].rearrange("p n t -> p (n t)").bitcast(I32))
-            return t
+            tile = keep.tile([P, TABLE], I32, name=name, tag=name, align_bytes=64)
+            nc.sync.dma_start(out=tile[:], in_=src[0].rearrange("p n t -> p (n t)").bitcast(I32))
+            return tile
 
         def load_scale_window(src, name, zero_engine):
-            t = keep.tile([P, TABLE], U8, name=name, align_bytes=64)
-            zero_engine.memset(t[:].bitcast(I32), 0)
-            nc.sync.dma_start(out=t[0:P:8, :].bitcast(I32), in_=src[0].bitcast(I32))
-            return t
+            tile = keep.tile([P, TABLE], U8, name=name, align_bytes=64)
+            zero_engine.memset(tile[:].bitcast(I32), 0)
+            nc.sync.dma_start(out=tile[0:P:BLOCK_PARTS, :].bitcast(I32), in_=src[0].bitcast(I32))
+            return tile
 
-        def place_scales(picked, plane, queue):
-            nc.vector.tensor_copy(out=plane[:].bitcast(I32), in_=picked[:].bitcast(I32))
-            for i in range(1, 4):
-                queue.dma_start(out=plane[i:P:32, :].bitcast(I32), in_=picked[8 * i : P : 32, :].bitcast(I32))
+        def move_scale_rows(picked, plane, first_row):
+            for i in range(first_row, ROWS_PER_QUADRANT):
+                nc.sync.dma_start(
+                    out=plane[i:P:QUADRANT, :].bitcast(I32),
+                    in_=picked[BLOCK_PARTS * i : P : QUADRANT, :].bitcast(I32),
+                )
 
         def entries(lst, first, count):
             return lst[:, first // PER_COL : (first + count) // PER_COL]
 
-        w1w_raw = keep.tile([P, 2 * H], U8, name="w1w_raw", align_bytes=64)
+        def pick_scales(dst, window, lst, first):
+            nc.vector.tensor_copy(out=dst, in_=window[:].indirect(entries(lst, first, PICK)))
+
+        def pick_words(window, lst, first, name, tag):
+            picked = keep.tile([P, PICK], I32, name=name, tag=tag, align_bytes=64)
+            nc.vector.tensor_copy(
+                out=picked[:].bitcast(U32), in_=window[:].bitcast(U32).indirect(entries(lst, first, PICK))
+            )
+            return picked
+
+        w1w_raw = keep.tile([P, FP4_BYTES * H], U8, name="w1w_raw", align_bytes=64)
         nc.sync.dma_start(out=w1w_raw[:].bitcast(I32), in_=w1_words[0].bitcast(I32))
         offs_t = load_list(offs, "offs_t")
         ka_t = load_list(ka, "ka_t")
@@ -71,8 +89,11 @@ def tile_picked_hdaqipagq_none_p_kernel(
         dw_win = load_words(d_words, "dw_win")
         w1s_raw = keep.tile([P, H], U8, name="w1s_raw", align_bytes=64)
         nc.vector.memset(w1s_raw[:].bitcast(I32), 0)
-        for i in range(4):
-            nc.sync.dma_start(out=w1s_raw[i:P:32, :].bitcast(I32), in_=w1_scales[0, i:16:4, :].bitcast(I32))
+        for i in range(ROWS_PER_QUADRANT):
+            nc.sync.dma_start(
+                out=w1s_raw[i:P:QUADRANT, :].bitcast(I32),
+                in_=w1_scales[0, i:SCALE_ROWS:ROWS_PER_QUADRANT, :].bitcast(I32),
+            )
         xw_win = load_words(x_words, "xw_win")
         gs4 = keep.tile([P, PACK], F32, name="gs4")
         nc.sync.dma_start(out=gs4[:], in_=gs.rearrange("(p t) o -> p (t o)", t=PACK))
@@ -80,18 +101,19 @@ def tile_picked_hdaqipagq_none_p_kernel(
         n3_t = load_list(n3, "n3_t")
         n2_t = load_list(n2, "n2_t")
 
-        w1w = keep.tile([P, 2 * H], U8, name="w1w", align_bytes=64)
+        w1w = keep.tile([P, FP4_BYTES * H], U8, name="w1w", align_bytes=64)
         nc.scalar.copy(
             out=w1w[:].bitcast(U16).rearrange("p (t m) -> p t m", t=PACK),
             in_=w1w_raw[:].bitcast(U16).rearrange("p (m t) -> p t m", t=PACK),
         )
 
-        picked0 = keep.tile([P, S + 2 * PICK], U8, name="picked0", tag="bytes_a", align_bytes=64)
-        nc.vector.tensor_copy(out=picked0[:, 0:S], in_=xs_win[:].indirect(offs_t[:]))
-        nc.vector.tensor_copy(out=picked0[:, S : S + PICK], in_=ds_win[:].indirect(entries(ka_t, 0, PICK)))
-        nc.vector.tensor_copy(out=picked0[:, S + PICK : S + 2 * PICK], in_=ds_win[:].indirect(entries(kb_t, 0, PICK)))
-        plane0 = keep.tile([P, S + 2 * PICK], U8, name="plane0", tag="bytes_b", align_bytes=64)
-        place_scales(picked0, plane0, nc.sync)
+        picked0 = keep.tile([P, S + 2 * PICK], U8, name="picked0", align_bytes=64)
+        pick_scales(picked0[:, 0:S], xs_win, offs_t, 0)
+        pick_scales(picked0[:, S : S + PICK], ds_win, ka_t, 0)
+        pick_scales(picked0[:, S + PICK : S + 2 * PICK], ds_win, kb_t, 0)
+        plane0 = keep.tile([P, S + 2 * PICK], U8, name="plane0", tag="plane0", align_bytes=64)
+        nc.vector.tensor_copy(out=plane0[:].bitcast(I32), in_=picked0[:].bitcast(I32))
+        move_scale_rows(picked0, plane0, 1)
 
         w1s = keep.tile([P, H], U8, name="w1s", align_bytes=64)
         nc.vector.tensor_copy(
@@ -99,15 +121,9 @@ def tile_picked_hdaqipagq_none_p_kernel(
             in_=w1s_raw[:].rearrange("p (m t) -> p t m", t=PACK),
         )
 
-        def pick_words(window, lst, first, name, tag):
-            picked = keep.tile([P, PICK], I32, name=name, tag=tag, align_bytes=64)
-            nc.vector.tensor_copy(out=picked[:].bitcast(U32), in_=window[:].bitcast(U32).indirect(entries(lst, first, PICK)))
-            return picked
-
-        ka_pick = pick_words(dw_win, ka_t, 0, "ka_pick0", "ka_pick")
+        ka_pick = pick_words(dw_win, ka_t, 0, "ka_pick0", "ka_pick0")
         xw_pick = pick_words(xw_win, offs_t, 0, "xw_pick", "xw_pick")
         kb_pick = pick_words(dw_win, kb_t, 0, "kb_pick0", "xw_win")
-        dw_pick = (ka_pick, kb_pick)
 
         pages = [keep.tile([P, U], F32, name=f"page{b}") for b in range(H // P)]
         hs = [keep.tile([P, S + PER_COL], F32, name=f"h{b}") for b in range(H // P)]
@@ -117,38 +133,38 @@ def tile_picked_hdaqipagq_none_p_kernel(
         zq = keep.tile([P, S], I32, name="zq", align_bytes=64)
         zs = keep.tile([P, S], U8, name="zs", align_bytes=64)
 
-        def second_product(acc, words, plane, first_scale, bb, cols):
+        def second_product(acc, words, plane, first_scale, block_in_set, cols):
             for m in range(2):
-                at = m * PICK + bb * P
+                at = first_scale + m * PICK + block_in_set * P
                 nc.tensor.matmul_mx(
                     out=acc[:],
-                    lhsT=words[m][:, bb * P : (bb + 1) * P].bitcast(FP8X4),
-                    lhsT_scale=plane[:, first_scale + at : first_scale + at + P],
+                    lhsT=words[m][:, block_in_set * P : (block_in_set + 1) * P].bitcast(FP8X4),
+                    lhsT_scale=plane[:, at : at + P],
                     rhs=zq[:, cols].bitcast(FP8X4),
                     rhs_scale=zs[:, cols],
                     start=(m == 0),
                     stop=(m == 1),
                 )
 
-        def finish(b):
+        def make_nw(b):
             fetched = keep.tile([P, S], F32, name=f"fetched{b}")
             nc.scalar.activation(out=fetched[:], in_=hs[b][:].indirect(n3_t[:]), func=COPY)
             nw = keep.tile([P, S], F32, name=f"nw{b}")
             nc.gpsimd.tensor_tensor(out=nw[:], in0=hs[b][:, 0:S], in1=fetched[:], op=SUBTRACT)
             return nw
 
-        def put_nw(b, nw):
+        def put_nw_and_store(b, nw):
             nc.scalar.activation(out=pages[b][:].indirect(n2_t[:]), in_=nw[:], func=COPY)
             nc.sync.dma_start(out=out[b * P : (b + 1) * P, :], in_=pages[b][:])
 
         ys = []
-        for hh in range(S // HALF):
-            cols = slice(hh * HALF, (hh + 1) * HALF)
-            y = psum.tile([P, PACK, HALF], F32, name=f"y{hh}")
+        for half in range(S // HALF):
+            cols = slice(half * HALF, (half + 1) * HALF)
+            y = psum.tile([P, PACK, HALF], F32, name=f"y{half}")
             for t in range(PACK):
                 nc.tensor.matmul_mx(
                     out=y[:, t, :],
-                    lhsT=w1w[:, 2 * P * t : 2 * P * (t + 1)].bitcast(FP4X4),
+                    lhsT=w1w[:, FP4_BYTES * P * t : FP4_BYTES * P * (t + 1)].bitcast(FP4X4),
                     lhsT_scale=w1s[:, P * t : P * (t + 1)],
                     rhs=xw_pick[:, cols].bitcast(FP8X4),
                     rhs_scale=plane0[:, cols],
@@ -156,45 +172,49 @@ def tile_picked_hdaqipagq_none_p_kernel(
                     stop=True,
                 )
             ys.append(y)
-        for hh in range(S // HALF):
-            cols = slice(hh * HALF, (hh + 1) * HALF)
-            zb = keep.tile([P, HALF * PACK], BF16, name=f"zb{hh}", tag="zb", align_bytes=64)
+
+        for half in range(S // HALF):
+            cols = slice(half * HALF, (half + 1) * HALF)
+            zb = keep.tile([P, HALF * PACK], BF16, name=f"zb{half}", tag="zb", align_bytes=64)
             nc.vector.tensor_tensor(
                 out=zb[:].rearrange("p (j t) -> p j t", t=PACK),
-                in0=ys[hh][:].rearrange("p t j -> p j t"),
+                in0=ys[half][:].rearrange("p t j -> p j t"),
                 in1=gs4[:].unsqueeze(1).to_broadcast([P, HALF, PACK]),
                 op=MULT,
             )
             nc.vector.quantize_mx(out=zq[:, cols].bitcast(FP8X4), scales=zs[:, cols], in_=zb[:])
-            for b in range(PICK // P):
-                acc = psum.tile([P, HALF], F32, name=f"acc{b}_{hh}")
-                second_product(acc, dw_pick, plane0, S, b, cols)
-                if hh == 0 and b == 0:
+            for b in range(BLOCKS_PER_SET):
+                acc = psum.tile([P, HALF], F32, name=f"acc{b}_{half}")
+                second_product(acc, (ka_pick, kb_pick), plane0, S, b, cols)
+                very_first = half == 0 and b == 0
+                if very_first:
                     nc.scalar.activation(out=hs[b][:, cols], in_=acc[:], func=COPY, scale=H_SCALE)
                 else:
                     nc.vector.tensor_scalar(out=hs[b][:, cols], in0=acc[:], scalar1=H_SCALE, scalar2=None, op0=MULT)
                 nc.scalar.activation(
-                    out=pages[b][:].indirect(entries(n1_t, hh * HALF, HALF)), in_=hs[b][:, cols], func=COPY
+                    out=pages[b][:].indirect(entries(n1_t, half * HALF, HALF)), in_=hs[b][:, cols], func=COPY
                 )
-        picked1 = keep.tile([P, 2 * PICK], U8, name="picked1", tag="bytes_b", align_bytes=64)
-        nc.vector.tensor_copy(out=picked1[:, 0:PICK], in_=ds_win[:].indirect(entries(ka_t, PICK, PICK)))
-        nc.vector.tensor_copy(out=picked1[:, PICK : 2 * PICK], in_=ds_win[:].indirect(entries(kb_t, PICK, PICK)))
-        plane1 = keep.tile([P, 2 * PICK], U8, name="plane1", tag="bytes_a", align_bytes=64)
-        place_scales(picked1, plane1, nc.sync)
-        nws = [finish(b) for b in range(PICK // P)]
-        for b in range(PICK // P):
-            put_nw(b, nws[b])
-        dw_pick = (
-            pick_words(dw_win, ka_t, PICK, "ka_pick1", "ka_pick"),
+
+        picked1 = keep.tile([P, 2 * PICK], U8, name="picked1", tag="ka_pick0", align_bytes=64)
+        pick_scales(picked1[:, 0:PICK], ds_win, ka_t, PICK)
+        pick_scales(picked1[:, PICK : 2 * PICK], ds_win, kb_t, PICK)
+        plane1 = keep.tile([P, 2 * PICK], U8, name="plane1", align_bytes=64)
+        nc.gpsimd.memset(plane1[:].bitcast(I32), 0)
+        move_scale_rows(picked1, plane1, 0)
+
+        nws = [make_nw(b) for b in range(BLOCKS_PER_SET)]
+        for b in range(BLOCKS_PER_SET):
+            put_nw_and_store(b, nws[b])
+
+        words1 = (
+            pick_words(dw_win, ka_t, PICK, "ka_pick1", "plane0"),
             pick_words(dw_win, kb_t, PICK, "kb_pick1", "xw_win"),
         )
-        nws = []
-        for bb in range(PICK // P):
-            b = PICK // P + bb
+        for b in range(BLOCKS_PER_SET, H // P):
             acc = psum.tile([P, S], F32, name=f"acc{b}")
-            second_product(acc, dw_pick, plane1, 0, bb, slice(0, S))
+            second_product(acc, words1, plane1, 0, b - BLOCKS_PER_SET, slice(0, S))
             nc.vector.tensor_scalar(out=hs[b][:, 0:S], in0=acc[:], scalar1=H_SCALE, scalar2=None, op0=MULT)
-            nws.append(finish(b))
+            nws.append(make_nw(b))
             nc.scalar.activation(out=pages[b][:].indirect(n1_t[:]), in_=hs[b][:, 0:S], func=COPY)
-        for bb in range(PICK // P):
-            put_nw(PICK // P + bb, nws[bb])
+        for b in range(BLOCKS_PER_SET, H // P):
+            put_nw_and_store(b, nws[b])

from contextlib import ExitStack

import concourse.mybir as mybir

F32 = mybir.dt.float32
BF16 = mybir.dt.bfloat16
I32 = mybir.dt.int32
U32 = mybir.dt.uint32
U16 = mybir.dt.uint16
U8 = mybir.dt.uint8
FP8X4 = mybir.dt.float8_e4m3fn_x4
FP4X4 = mybir.dt.float4_e2m1fn_x4
COPY = mybir.ActivationFunctionType.Copy
MULT = mybir.AluOpType.mult
SUBTRACT = mybir.AluOpType.subtract

P = 128
PACK = 4
K = 512
TABLE = 2048
S = 256
H = 512
U = 512
PER_COL = 16
QUADRANT = 32
ROWS_PER_QUADRANT = 4
SCALE_ROWS = 16
BLOCK_PARTS = 8
FP4_BYTES = 2
HALF = 128
PICK = 256
BLOCKS_PER_SET = PICK // P
H_SCALE = 0.0625

FLOPS = 2 * K * H * S * 3


def tile_picked_hdaqipagq_none_p_kernel(
    tc, x_words, x_scales, w1_words, w1_scales, gs, d_words, d_scales, offs, ka, kb, n1, n2, n3, out
):
    nc = tc.nc
    with ExitStack() as ctx:
        keep = ctx.enter_context(tc.tile_pool(name="keep", bufs=1))
        psum = ctx.enter_context(tc.psum_pool(name="psum", bufs=1))

        def load_list(src, name):
            tile = keep.tile(list(src.shape), U16, name=name)
            nc.sync.dma_start(out=tile[:], in_=src)
            return tile

        def load_words(src, name):
            tile = keep.tile([P, TABLE], I32, name=name, tag=name, align_bytes=64)
            nc.sync.dma_start(out=tile[:], in_=src[0].rearrange("p n t -> p (n t)").bitcast(I32))
            return tile

        def load_scale_window(src, name, zero_engine):
            tile = keep.tile([P, TABLE], U8, name=name, align_bytes=64)
            zero_engine.memset(tile[:].bitcast(I32), 0)
            nc.sync.dma_start(out=tile[0:P:BLOCK_PARTS, :].bitcast(I32), in_=src[0].bitcast(I32))
            return tile

        def move_scale_rows(picked, plane, first_row):
            for i in range(first_row, ROWS_PER_QUADRANT):
                nc.sync.dma_start(
                    out=plane[i:P:QUADRANT, :].bitcast(I32),
                    in_=picked[BLOCK_PARTS * i : P : QUADRANT, :].bitcast(I32),
                )

        def entries(lst, first, count):
            return lst[:, first // PER_COL : (first + count) // PER_COL]

        def pick_scales(dst, window, lst, first):
            nc.vector.tensor_copy(out=dst, in_=window[:].indirect(entries(lst, first, PICK)))

        def pick_words(window, lst, first, name, tag):
            picked = keep.tile([P, PICK], I32, name=name, tag=tag, align_bytes=64)
            nc.vector.tensor_copy(
                out=picked[:].bitcast(U32), in_=window[:].bitcast(U32).indirect(entries(lst, first, PICK))
            )
            return picked

        w1w_raw = keep.tile([P, FP4_BYTES * H], U8, name="w1w_raw", align_bytes=64)
        nc.sync.dma_start(out=w1w_raw[:].bitcast(I32), in_=w1_words[0].bitcast(I32))
        offs_t = load_list(offs, "offs_t")
        ka_t = load_list(ka, "ka_t")
        kb_t = load_list(kb, "kb_t")
        xs_win = load_scale_window(x_scales, "xs_win", nc.vector)
        ds_win = load_scale_window(d_scales, "ds_win", nc.gpsimd)
        dw_win = load_words(d_words, "dw_win")
        w1s_raw = keep.tile([P, H], U8, name="w1s_raw", align_bytes=64)
        nc.vector.memset(w1s_raw[:].bitcast(I32), 0)
        for i in range(ROWS_PER_QUADRANT):
            nc.sync.dma_start(
                out=w1s_raw[i:P:QUADRANT, :].bitcast(I32),
                in_=w1_scales[0, i:SCALE_ROWS:ROWS_PER_QUADRANT, :].bitcast(I32),
            )
        xw_win = load_words(x_words, "xw_win")
        gs4 = keep.tile([P, PACK], F32, name="gs4")
        nc.sync.dma_start(out=gs4[:], in_=gs.rearrange("(p t) o -> p (t o)", t=PACK))
        n1_t = load_list(n1, "n1_t")
        n3_t = load_list(n3, "n3_t")
        n2_t = load_list(n2, "n2_t")

        w1w = keep.tile([P, FP4_BYTES * H], U8, name="w1w", align_bytes=64)
        nc.scalar.copy(
            out=w1w[:].bitcast(U16).rearrange("p (t m) -> p t m", t=PACK),
            in_=w1w_raw[:].bitcast(U16).rearrange("p (m t) -> p t m", t=PACK),
        )

        picked0 = keep.tile([P, S + 2 * PICK], U8, name="picked0", align_bytes=64)
        pick_scales(picked0[:, 0:S], xs_win, offs_t, 0)
        pick_scales(picked0[:, S : S + PICK], ds_win, ka_t, 0)
        pick_scales(picked0[:, S + PICK : S + 2 * PICK], ds_win, kb_t, 0)
        plane0 = keep.tile([P, S + 2 * PICK], U8, name="plane0", tag="plane0", align_bytes=64)
        nc.vector.tensor_copy(out=plane0[:].bitcast(I32), in_=picked0[:].bitcast(I32))
        move_scale_rows(picked0, plane0, 1)

        w1s = keep.tile([P, H], U8, name="w1s", align_bytes=64)
        nc.vector.tensor_copy(
            out=w1s[:].rearrange("p (t m) -> p t m", t=PACK),
            in_=w1s_raw[:].rearrange("p (m t) -> p t m", t=PACK),
        )

        ka_pick = pick_words(dw_win, ka_t, 0, "ka_pick0", "ka_pick0")
        xw_pick = pick_words(xw_win, offs_t, 0, "xw_pick", "xw_pick")
        kb_pick = pick_words(dw_win, kb_t, 0, "kb_pick0", "xw_win")

        pages = [keep.tile([P, U], F32, name=f"page{b}") for b in range(H // P)]
        hs = [keep.tile([P, S + PER_COL], F32, name=f"h{b}") for b in range(H // P)]
        for h in hs:
            nc.gpsimd.memset(h[:, S : S + PER_COL], 0.0)

        zq = keep.tile([P, S], I32, name="zq", align_bytes=64)
        zs = keep.tile([P, S], U8, name="zs", align_bytes=64)

        def second_product(acc, words, plane, first_scale, block_in_set, cols):
            for m in range(2):
                at = first_scale + m * PICK + block_in_set * P
                nc.tensor.matmul_mx(
                    out=acc[:],
                    lhsT=words[m][:, block_in_set * P : (block_in_set + 1) * P].bitcast(FP8X4),
                    lhsT_scale=plane[:, at : at + P],
                    rhs=zq[:, cols].bitcast(FP8X4),
                    rhs_scale=zs[:, cols],
                    start=(m == 0),
                    stop=(m == 1),
                )

        def make_nw(b):
            fetched = keep.tile([P, S], F32, name=f"fetched{b}")
            nc.scalar.activation(out=fetched[:], in_=hs[b][:].indirect(n3_t[:]), func=COPY)
            nw = keep.tile([P, S], F32, name=f"nw{b}")
            nc.gpsimd.tensor_tensor(out=nw[:], in0=hs[b][:, 0:S], in1=fetched[:], op=SUBTRACT)
            return nw

        def put_nw_and_store(b, nw):
            nc.scalar.activation(out=pages[b][:].indirect(n2_t[:]), in_=nw[:], func=COPY)
            nc.sync.dma_start(out=out[b * P : (b + 1) * P, :], in_=pages[b][:])

        ys = []
        for half in range(S // HALF):
            cols = slice(half * HALF, (half + 1) * HALF)
            y = psum.tile([P, PACK, HALF], F32, name=f"y{half}")
            for t in range(PACK):
                nc.tensor.matmul_mx(
                    out=y[:, t, :],
                    lhsT=w1w[:, FP4_BYTES * P * t : FP4_BYTES * P * (t + 1)].bitcast(FP4X4),
                    lhsT_scale=w1s[:, P * t : P * (t + 1)],
                    rhs=xw_pick[:, cols].bitcast(FP8X4),
                    rhs_scale=plane0[:, cols],
                    start=True,
                    stop=True,
                )
            ys.append(y)

        for half in range(S // HALF):
            cols = slice(half * HALF, (half + 1) * HALF)
            zb = keep.tile([P, HALF * PACK], BF16, name=f"zb{half}", tag="zb", align_bytes=64)
            nc.vector.tensor_tensor(
                out=zb[:].rearrange("p (j t) -> p j t", t=PACK),
                in0=ys[half][:].rearrange("p t j -> p j t"),
                in1=gs4[:].unsqueeze(1).to_broadcast([P, HALF, PACK]),
                op=MULT,
            )
            nc.vector.quantize_mx(out=zq[:, cols].bitcast(FP8X4), scales=zs[:, cols], in_=zb[:])
            for b in range(BLOCKS_PER_SET):
                acc = psum.tile([P, HALF], F32, name=f"acc{b}_{half}")
                second_product(acc, (ka_pick, kb_pick), plane0, S, b, cols)
                very_first = half == 0 and b == 0
                if very_first:
                    nc.scalar.activation(out=hs[b][:, cols], in_=acc[:], func=COPY, scale=H_SCALE)
                else:
                    nc.vector.tensor_scalar(out=hs[b][:, cols], in0=acc[:], scalar1=H_SCALE, scalar2=None, op0=MULT)
                nc.scalar.activation(
                    out=pages[b][:].indirect(entries(n1_t, half * HALF, HALF)), in_=hs[b][:, cols], func=COPY
                )

        picked1 = keep.tile([P, 2 * PICK], U8, name="picked1", tag="ka_pick0", align_bytes=64)
        pick_scales(picked1[:, 0:PICK], ds_win, ka_t, PICK)
        pick_scales(picked1[:, PICK : 2 * PICK], ds_win, kb_t, PICK)
        plane1 = keep.tile([P, 2 * PICK], U8, name="plane1", align_bytes=64)
        nc.gpsimd.memset(plane1[:].bitcast(I32), 0)
        move_scale_rows(picked1, plane1, 0)

        nws = [make_nw(b) for b in range(BLOCKS_PER_SET)]
        for b in range(BLOCKS_PER_SET):
            put_nw_and_store(b, nws[b])

        words1 = (
            pick_words(dw_win, ka_t, PICK, "ka_pick1", "plane0"),
            pick_words(dw_win, kb_t, PICK, "kb_pick1", "xw_win"),
        )
        for b in range(BLOCKS_PER_SET, H // P):
            acc = psum.tile([P, S], F32, name=f"acc{b}")
            second_product(acc, words1, plane1, 0, b - BLOCKS_PER_SET, slice(0, S))
            nc.vector.tensor_scalar(out=hs[b][:, 0:S], in0=acc[:], scalar1=H_SCALE, scalar2=None, op0=MULT)
            nws.append(make_nw(b))
            nc.scalar.activation(out=pages[b][:].indirect(n1_t[:]), in_=hs[b][:, 0:S], func=COPY)
        for b in range(BLOCKS_PER_SET, H // P):
            put_nw_and_store(b, nws[b])
